import numpy as np
import ml_dtypes


def mxq(x, axis, fmt="e4m3"):
    dtype, down = {"e4m3": (ml_dtypes.float8_e4m3fn, 7), "e5m2": (ml_dtypes.float8_e5m2, 14)}[fmt]
    v = np.moveaxis(np.asarray(x, np.float32).astype(ml_dtypes.bfloat16).astype(np.float64), axis, -1)
    blocks = v.reshape(v.shape[:-1] + (-1, 32))
    amax = np.abs(blocks).max(-1, keepdims=True)
    byte = np.maximum(np.where(amax > 0, np.frexp(amax)[1] - 1 + 127, 0) - down, 1)
    scale = np.exp2(byte - 127.0)
    codes = (blocks / scale).astype(np.float32).astype(dtype).astype(np.float64)
    return np.moveaxis((codes * scale).reshape(v.shape), -1, axis)


WIDE = False


def mx_kscale(k):
    if not WIDE:
        return np.ones(k)
    levels = np.array([10, -10, 5, -5, 0])
    if k % 512:
        return np.exp2(np.random.permutation(np.resize(levels, k // 32))).repeat(32)
    a = np.empty((k // 512, 16))
    for p in range(k // 512):
        a[p, :8] = np.random.permutation(np.resize(levels, 8))
        for g in range(8):
            far = levels[np.abs(levels - a[p, g]) >= 10]
            a[p, g + 8] = far[np.random.randint(len(far))]
    return np.exp2(a.ravel()).repeat(32)


def f64(x):
    return np.asarray(x).astype(np.float64)


def striped(idx):
    return np.tile(np.asarray(idx).reshape(-1, 16).T, (8, 1)).astype(np.uint16)


def unstriped(offs):
    return offs[:16].T.reshape(-1).astype(np.int64)


B, N, T, D, DV, NQ = 2, 512, 2048, 512, 256, 128


def setup_inputs():
    n = np.random.standard_normal
    seg = T // B
    idx = np.concatenate([b * seg + np.random.permutation(seg)[:N] for b in range(B)])
    s = mx_kscale(D)[:, None]
    u = np.ones(T)
    u[idx] = mx_kscale(B * N)
    r = np.random.uniform(0.5, 2.0, T)
    k = n((D, T)) / s
    v = n((DV, T)) / (u * r)
    return {
        "qT": (n((B, D, NQ)) * s * (0.80 / np.sqrt(D))).astype(np.float32),
        "kT": k.astype(np.float32),
        "vT": v.astype(np.float32),
        "vs": np.tile(u * r, (128, 1)).astype(np.float32),
        "offs": striped(idx),
    }


def reference(qT, kT, vT, vs, offs):
    idx = unstriped(offs)
    k = f64(kT)
    v = f64(vT)
    pick = lambda x: x[:, idx].reshape(x.shape[0], B, N).transpose(1, 0, 2)
    q = f64(qT)
    score = mxq(q, 1, "e4m3").transpose(0, 2, 1) @ mxq(pick(k), 1, "e4m3")
    p = np.square(np.maximum(score, 0.0))
    total = p.sum(-1, keepdims=True) + 1.0
    w = p * pick(f64(vs))[:, :1, :]
    y = mxq(w, 2, "e4m3") @ mxq(pick(v).transpose(0, 2, 1), 1, "e4m3")
    y = y / total
    return y

@@ -1,0 +1,226 @@
+from contextlib import ExitStack
+
+import concourse.mybir as mybir
+from concourse.masks import make_identity
+
+B, NQ, N, T, D, DV = 2, 128, 512, 2048, 512, 256
+P = 128
+PACK = 4
+SEG = T // B
+HALF = DV // 2
+
+F32 = mybir.dt.float32
+BF16 = mybir.dt.bfloat16
+U32 = mybir.dt.uint32
+U16 = mybir.dt.uint16
+U8 = mybir.dt.uint8
+FP8X4 = mybir.dt.float8_e4m3fn_x4
+COPY = mybir.ActivationFunctionType.Copy
+RELU = mybir.ActivationFunctionType.Relu
+SQUARE = mybir.ActivationFunctionType.Square
+ADD = mybir.AluOpType.add
+MAX = mybir.AluOpType.max
+MULT = mybir.AluOpType.mult
+
+FLOPS = 2 * B * NQ * N * (D + DV)
+BYTES = 4 * (B * D * NQ + D * T + DV * T + T + B * NQ * DV) + 2 * P * (B * N // 16)
+
+
+def tile_attend_relu2_seg_kernel(tc, qT, kT, vT, vs, offs, out):
+    nc = tc.nc
+    with ExitStack() as ctx:
+        keep = ctx.enter_context(tc.tile_pool(name="keep", bufs=1))
+        turn_pool = ctx.enter_context(tc.psum_pool(name="turns", bufs=4))
+        score_pool = ctx.enter_context(tc.psum_pool(name="scores", bufs=2))
+        y_pool = ctx.enter_context(tc.psum_pool(name="ys", bufs=2))
+
+        offsets = keep.tile([P, B * N // 16], U16, name="offsets")
+        vs_tab = keep.tile([P, T], F32, name="vs_tab")
+        ident = keep.tile([P, P], F32, name="ident")
+        warm = keep.tile([P, 8], F32, name="warm")
+        q_raw = keep.tile([P, B, PACK * NQ], F32, name="q_raw")
+        v_raw = [keep.tile([P, T], F32, name="v_raw%d" % h) for h in range(2)]
+        k_raw = [[keep.tile([P, 2, SEG], F32, name="k_raw%d%d" % (u, b)) for b in range(B)] for u in range(2)]
+        k_pairs = [keep.tile([P, T, 2], BF16, name="k_pairs%d" % u, align_bytes=64) for u in range(2)]
+
+        nc.vector.memset(vs_tab[:, 0 : T // 2], 0.0)
+        nc.gpsimd.memset(vs_tab[:, T // 2 : T], 0.0)
+        nc.vector.memset(warm[:], 0.0)
+        make_identity(nc, ident[:])
+        nc.scalar.activation(warm[:, 4:8], warm[:, 0:4], SQUARE)
+
+        kv = kT.rearrange("(p j) n -> p j n", j=PACK)
+        nc.sync.dma_start(offsets[:], offs)
+        nc.sync.dma_start(q_raw[:], qT.rearrange("b (p j) q -> p b (j q)", j=PACK))
+        nc.sync.dma_start(v_raw[0][:, 0:SEG], vT[0:P, 0:SEG])
+        nc.sync.dma_start(vs_tab[0:1, :], vs[0:1, :])
+        nc.sync.dma_start(v_raw[1][:, 0:SEG], vT[P : 2 * P, 0:SEG])
+        for b in range(B):
+            for u in range(2):
+                for c in range(2):
+                    a0 = c * (SEG // 2)
+                    a1 = a0 + SEG // 2
+                    nc.sync.dma_start(
+                        k_raw[u][b][:, :, a0:a1], kv[:, 2 * u : 2 * u + 2, b * SEG + a0 : b * SEG + a1]
+                    )
+        for h in range(2):
+            nc.sync.dma_start(v_raw[h][:, SEG:T], vT[h * P : (h + 1) * P, SEG:T])
+
+        def listed(b):
+            return offsets[:, b * (N // 16) : (b + 1) * (N // 16)]
+
+        q_in = keep.tile([P, B, NQ, PACK], BF16, name="q_in", align_bytes=64)
+        q_codes = keep.tile([P, B * NQ], U32, name="q_codes", align_bytes=64)
+        q_scales = keep.tile([P, B * NQ], U8, name="q_scales", align_bytes=64)
+        for b in range(B):
+            nc.scalar.activation(q_in[:, b, :, :], q_raw[:, b, :].rearrange("p (j q) -> p q j", j=PACK), COPY)
+        nc.vector.quantize_mx(
+            out=q_codes[:].bitcast(FP8X4), scales=q_scales[:], in_=q_in[:].rearrange("p b q j -> p (b q j)")
+        )
+
+        vs_cols = [keep.tile([P, PACK], F32, name="vs_cols%d" % b) for b in range(B)]
+
+        def scales_of(b):
+            g = keep.tile([P, N], F32, name="vs_got%d" % b)
+            nc.vector.tensor_copy(g[:], vs_tab[:].indirect(listed(b)))
+            turned = turn_pool.tile([P, PACK, P], F32, name="turned")
+            for t in range(PACK):
+                nc.tensor.transpose(turned[:, t, :], g[:, t:N:PACK], ident[:])
+            nc.vector.tensor_copy(vs_cols[b][:], turned[:, :, 0])
+
+        v_codes = [keep.tile([P, DV], U32, name="v_codes%d" % b, align_bytes=64) for b in range(B)]
+        v_scales = [keep.tile([P, DV], U8, name="v_scales%d" % b, align_bytes=64) for b in range(B)]
+        v_in = [keep.tile([P, DV, PACK], BF16, name="v_in%d" % b, align_bytes=64) for b in range(B)]
+
+        def values_turned(b, h):
+            g = keep.tile([P, N], F32, name="v_got%d%d" % (b, h))
+            window = v_raw[h][:, 0:SEG] if b == 0 else v_raw[h][:]
+            nc.vector.tensor_copy(g[:], window.indirect(listed(b)))
+            turned = turn_pool.tile([P, PACK, P], F32, name="turned")
+            for t in range(PACK):
+                nc.tensor.transpose(turned[:, t, :], g[:, t:N:PACK], ident[:])
+            nc.scalar.activation(
+                v_in[b][:, h * HALF : (h + 1) * HALF, :], turned[:].rearrange("s t e -> s e t"), COPY
+            )
+
+        def values_quantized(b, e0, e1):
+            nc.vector.quantize_mx(
+                out=v_codes[b][:, e0:e1].bitcast(FP8X4),
+                scales=v_scales[b][:, e0:e1],
+                in_=v_in[b][:, e0:e1, :].rearrange("s e t -> s (e t)"),
+            )
+
+        k_in = [keep.tile([P, PACK, P, 2], U32, name="k_in%d" % b, align_bytes=64) for b in range(B)]
+        k_codes = [keep.tile([P, N], U32, name="k_codes%d" % b, align_bytes=64) for b in range(B)]
+        k_scales = [keep.tile([P, N], U8, name="k_scales%d" % b, align_bytes=64) for b in range(B)]
+
+        def keys_cast(engine, u, b, a0, a1):
+            dst = k_pairs[u][:, b * SEG + a0 : b * SEG + a1, :]
+            source = k_raw[u][b][:, :, a0:a1].rearrange("p e n -> p n e")
+            if engine == "scalar":
+                nc.scalar.activation(dst, source, COPY)
+            else:
+                nc.vector.tensor_copy(dst, source)
+
+        def keys_got(u, b):
+            words = k_pairs[u][:].rearrange("p n e -> p (n e)").bitcast(U32)
+            window = words[:, 0:SEG] if b == 0 else words
+            nc.vector.tensor_copy(k_in[b][:, :, :, u].rearrange("p t s -> p s t"), window.indirect(listed(b)))
+
+        def keys_quantized(b):
+            nc.vector.quantize_mx(
+                out=k_codes[b][:].bitcast(FP8X4),
+                scales=k_scales[b][:],
+                in_=k_in[b][:].rearrange("p t s u -> p (t s u)").bitcast(BF16),
+            )
+
+        recip = [keep.tile([P, 1], F32, name="recip%d" % b) for b in range(B)]
+        w_codes = [keep.tile([P, NQ], U32, name="w_codes%d" % b, align_bytes=64) for b in range(B)]
+        w_scales = [keep.tile([P, NQ], U8, name="w_scales%d" % b, align_bytes=64) for b in range(B)]
+
+        def weights(b):
+            scores = score_pool.tile([P, PACK, NQ], F32, name="scores")
+            for t in range(PACK):
+                nc.tensor.matmul_mx(
+                    out=scores[:, t, :],
+                    lhsT=k_codes[b][:, t * P : (t + 1) * P].bitcast(FP8X4),
+                    lhsT_scale=k_scales[b][:, t * P : (t + 1) * P],
+                    rhs=q_codes[:, b * NQ : (b + 1) * NQ].bitcast(FP8X4),
+                    rhs_scale=q_scales[:, b * NQ : (b + 1) * NQ],
+                    start=True,
+                    stop=True,
+                )
+            scaled = keep.tile([P, PACK, NQ], F32, name="scaled%d" % b)
+            for t in range(PACK):
+                nc.scalar.activation(scaled[:, t, :], scores[:, t, :], COPY, scale=vs_cols[b][:, t : t + 1])
+            w_in = keep.tile([P, NQ, PACK], BF16, name="w_in%d" % b, align_bytes=64)
+            nc.vector.scalar_tensor_tensor(
+                out=w_in[:],
+                in0=scores[:].rearrange("s t q -> s q t"),
+                scalar=0.0,
+                in1=scaled[:].rearrange("s t q -> s q t"),
+                op0=MAX,
+                op1=MULT,
+            )
+            nc.vector.quantize_mx(
+                out=w_codes[b][:].bitcast(FP8X4), scales=w_scales[b][:], in_=w_in[:].rearrange("s q t -> s (q t)")
+            )
+            positive = keep.tile([P, PACK, NQ], F32, name="positive%d" % b)
+            nc.scalar.activation(positive[:], scores[:], RELU)
+            turned = turn_pool.tile([P, PACK, P], F32, name="turned")
+            for t in range(PACK):
+                nc.tensor.transpose(turned[:, t, :], positive[:, t, :], ident[:])
+            squares = keep.tile([P, PACK, P], F32, name="squares%d" % b)
+            total = keep.tile([P, 1], F32, name="total%d" % b)
+            nc.scalar.activation(squares[:], turned[:], SQUARE, accum_out=total[:])
+            total1 = keep.tile([P, 1], F32, name="total1%d" % b)
+            nc.vector.tensor_scalar(total1[:], total[:], 1.0, None, op0=ADD)
+            nc.vector.reciprocal(recip[b][:], total1[:])
+
+        y_sb = [keep.tile([P, DV], F32, name="y_sb%d" % b) for b in range(B)]
+
+        def outputs(b, e0, e1):
+            y = y_pool.tile([P, DV], F32, name="y")
+            nc.tensor.matmul_mx(
+                out=y[:, 0 : e1 - e0],
+                lhsT=w_codes[b][:].bitcast(FP8X4),
+                lhsT_scale=w_scales[b][:],
+                rhs=v_codes[b][:, e0:e1].bitcast(FP8X4),
+                rhs_scale=v_scales[b][:, e0:e1],
+                start=True,
+                stop=True,
+            )
+            nc.scalar.activation(y_sb[b][:, e0:e1], y[:, 0 : e1 - e0], COPY, scale=recip[b][:])
+            nc.sync.dma_start(out[b][:, e0:e1], y_sb[b][:, e0:e1])
+
+        H = SEG // 2
+        values_turned(0, 0)
+        scales_of(0)
+        values_turned(0, 1)
+        keys_cast("scalar", 0, 0, 0, H)
+        keys_cast("scalar", 0, 0, H, SEG)
+        keys_got(0, 0)
+        values_quantized(0, 0, DV)
+        keys_cast("scalar", 1, 0, 0, H)
+        keys_cast("scalar", 1, 0, H, H + 192)
+        keys_cast("vector", 1, 0, H + 192, SEG)
+        keys_got(1, 0)
+        keys_quantized(0)
+        scales_of(1)
+        keys_cast("scalar", 0, 1, 0, H)
+        keys_cast("scalar", 0, 1, H, SEG)
+        weights(0)
+        keys_got(0, 1)
+        outputs(0, 0, DV)
+        keys_cast("scalar", 1, 1, 0, H)
+        keys_cast("scalar", 1, 1, H, H + 192)
+        keys_cast("vector", 1, 1, H + 192, SEG)
+        keys_got(1, 1)
+        keys_quantized(1)
+        values_turned(1, 0)
+        weights(1)
+        values_quantized(1, 0, HALF)
+        values_turned(1, 1)
+        values_quantized(1, HALF, DV)
+        outputs(1, 0, HALF)
+        outputs(1, HALF, DV)

@@ -39,106 +39,163 @@ def tile_attend_relu2_seg_kernel(tc, qT, kT, vT, vs, offs, out):
         ident = keep.tile([P, P], F32, name="ident")
         warm = keep.tile([P, 8], F32, name="warm")
         q_raw = keep.tile([P, B, PACK * NQ], F32, name="q_raw")
-        v_raw = [keep.tile([P, T], F32, name="v_raw%d" % h) for h in range(2)]
-        k_raw = [[keep.tile([P, 2, SEG], F32, name="k_raw%d%d" % (u, b)) for b in range(B)] for u in range(2)]
+        v_raw = keep.tile([P, 2, T], F32, name="v_raw")
+        k_raw = [[keep.tile([P, 2, SEG], F32, name="k_raw%d%d" % (u, b)) for u in range(2)] for b in range(B)]
         k_pairs = [keep.tile([P, T, 2], BF16, name="k_pairs%d" % u, align_bytes=64) for u in range(2)]
-
-        nc.vector.memset(vs_tab[:, 0 : T // 2], 0.0)
-        nc.gpsimd.memset(vs_tab[:, T // 2 : T], 0.0)
-        nc.vector.memset(warm[:], 0.0)
-        make_identity(nc, ident[:])
-        nc.scalar.activation(warm[:, 4:8], warm[:, 0:4], SQUARE)
-
+        q_in = keep.tile([P, B, NQ, PACK], BF16, name="q_in", align_bytes=64)
+        q_codes = keep.tile([P, B * NQ], U32, name="q_codes", align_bytes=64)
+        q_scales = keep.tile([P, B * NQ], U8, name="q_scales", align_bytes=64)
+        vs_got = keep.tile([P, B * N], F32, name="vs_got")
+        vs_cols = keep.tile([P, B * PACK], F32, name="vs_cols")
+        v_pairs = keep.tile([P, T, 2], BF16, name="v_pairs", align_bytes=64)
+        v_words = [keep.tile([P, PACK, P], U32, name="v_words%d" % b, align_bytes=64) for b in range(B)]
+        v_got = [[keep.tile([P, N], F32, name="v_got%d%d" % (b, h)) for h in range(2)] for b in range(B)]
+        v_codes = [keep.tile([P, DV], U32, name="v_codes%d" % b, align_bytes=64) for b in range(B)]
+        v_scales = [keep.tile([P, DV], U8, name="v_scales%d" % b, align_bytes=64) for b in range(B)]
+        v_in = [keep.tile([P, DV, PACK], BF16, name="v_in%d" % b, align_bytes=64) for b in range(B)]
+        k_in = [keep.tile([P, PACK, P, 2], U32, name="k_in%d" % b, align_bytes=64) for b in range(B)]
+        k_codes = [keep.tile([P, N], U32, name="k_codes%d" % b, align_bytes=64) for b in range(B)]
+        k_scales = [keep.tile([P, N], U8, name="k_scales%d" % b, align_bytes=64) for b in range(B)]
+        scaled = [keep.tile([P, PACK, NQ], F32, name="scaled%d" % b) for b in range(B)]
+        positive = [keep.tile([P, PACK, NQ], F32, name="positive%d" % b) for b in range(B)]
+        squares = [keep.tile([P, PACK, P], F32, name="squares%d" % b) for b in range(B)]
+        w_in = [keep.tile([P, NQ, PACK], BF16, name="w_in%d" % b, align_bytes=64) for b in range(B)]
+        w_codes = [keep.tile([P, NQ], U32, name="w_codes%d" % b, align_bytes=64) for b in range(B)]
+        w_scales = [keep.tile([P, NQ], U8, name="w_scales%d" % b, align_bytes=64) for b in range(B)]
+        total = [keep.tile([P, 1], F32, name="total%d" % b) for b in range(B)]
+        total1 = [keep.tile([P, 1], F32, name="total1%d" % b) for b in range(B)]
+        recip = [keep.tile([P, 1], F32, name="recip%d" % b) for b in range(B)]
+        y_sb = [keep.tile([P, DV], F32, name="y_sb%d" % b) for b in range(B)]
+        bank = {}
         kv = kT.rearrange("(p j) n -> p j n", j=PACK)
-        nc.sync.dma_start(offsets[:], offs)
-        nc.sync.dma_start(q_raw[:], qT.rearrange("b (p j) q -> p b (j q)", j=PACK))
-        nc.sync.dma_start(v_raw[0][:, 0:SEG], vT[0:P, 0:SEG])
-        nc.sync.dma_start(vs_tab[0:1, :], vs[0:1, :])
-        nc.sync.dma_start(v_raw[1][:, 0:SEG], vT[P : 2 * P, 0:SEG])
-        for b in range(B):
-            for u in range(2):
-                for c in range(2):
-                    a0 = c * (SEG // 2)
-                    a1 = a0 + SEG // 2
-                    nc.sync.dma_start(
-                        k_raw[u][b][:, :, a0:a1], kv[:, 2 * u : 2 * u + 2, b * SEG + a0 : b * SEG + a1]
-                    )
-        for h in range(2):
-            nc.sync.dma_start(v_raw[h][:, SEG:T], vT[h * P : (h + 1) * P, SEG:T])
 
         def listed(b):
             return offsets[:, b * (N // 16) : (b + 1) * (N // 16)]
 
-        q_in = keep.tile([P, B, NQ, PACK], BF16, name="q_in", align_bytes=64)
-        q_codes = keep.tile([P, B * NQ], U32, name="q_codes", align_bytes=64)
-        q_scales = keep.tile([P, B * NQ], U8, name="q_scales", align_bytes=64)
-        for b in range(B):
+        def load_scales():
+            nc.sync.dma_start(vs_tab[0:1, :], vs[0:1, :])
+
+        def load_queries():
+            nc.sync.dma_start(q_raw[:], qT.rearrange("b (p j) q -> p b (j q)", j=PACK))
+
+        def load_values(b, h):
+            nc.sync.dma_start(v_raw[:, h, b * SEG : (b + 1) * SEG], vT[h * P : (h + 1) * P, b * SEG : (b + 1) * SEG])
+
+        def load_keys(b, u, c):
+            a0, a1 = (0, SEG) if c is None else (c * (SEG // 2), (c + 1) * (SEG // 2))
+            nc.sync.dma_start(k_raw[b][u][:, :, a0:a1], kv[:, 2 * u : 2 * u + 2, b * SEG + a0 : b * SEG + a1])
+
+        def cast_queries(b):
             nc.scalar.activation(q_in[:, b, :, :], q_raw[:, b, :].rearrange("p (j q) -> p q j", j=PACK), COPY)
-        nc.vector.quantize_mx(
-            out=q_codes[:].bitcast(FP8X4), scales=q_scales[:], in_=q_in[:].rearrange("p b q j -> p (b q j)")
-        )
 
-        vs_cols = [keep.tile([P, PACK], F32, name="vs_cols%d" % b) for b in range(B)]
+        def cast_queries_gpsimd():
+            for b in range(B):
+                nc.gpsimd.tensor_scalar(
+                    q_in[:, b, :, :], q_raw[:, b, :].rearrange("p (j q) -> p q j", j=PACK), 1.0, 0.0, op0=MULT, op1=ADD
+                )
 
-        def scales_of(b):
-            g = keep.tile([P, N], F32, name="vs_got%d" % b)
-            nc.vector.tensor_copy(g[:], vs_tab[:].indirect(listed(b)))
-            turned = turn_pool.tile([P, PACK, P], F32, name="turned")
-            for t in range(PACK):
-                nc.tensor.transpose(turned[:, t, :], g[:, t:N:PACK], ident[:])
-            nc.vector.tensor_copy(vs_cols[b][:], turned[:, :, 0])
-
-        v_codes = [keep.tile([P, DV], U32, name="v_codes%d" % b, align_bytes=64) for b in range(B)]
-        v_scales = [keep.tile([P, DV], U8, name="v_scales%d" % b, align_bytes=64) for b in range(B)]
-        v_in = [keep.tile([P, DV, PACK], BF16, name="v_in%d" % b, align_bytes=64) for b in range(B)]
-
-        def values_turned(b, h):
-            g = keep.tile([P, N], F32, name="v_got%d%d" % (b, h))
-            window = v_raw[h][:, 0:SEG] if b == 0 else v_raw[h][:]
-            nc.vector.tensor_copy(g[:], window.indirect(listed(b)))
-            turned = turn_pool.tile([P, PACK, P], F32, name="turned")
-            for t in range(PACK):
-                nc.tensor.transpose(turned[:, t, :], g[:, t:N:PACK], ident[:])
-            nc.scalar.activation(
-                v_in[b][:, h * HALF : (h + 1) * HALF, :], turned[:].rearrange("s t e -> s e t"), COPY
+        def quantize_queries():
+            nc.vector.quantize_mx(
+                out=q_codes[:].bitcast(FP8X4), scales=q_scales[:], in_=q_in[:].rearrange("p b q j -> p (b q j)")
             )
 
-        def values_quantized(b, e0, e1):
+        def gather_scales():
+            nc.vector.tensor_copy(vs_got[:], vs_tab[:].indirect(offsets[:]))
+
+        def turn(key, source):
+            turned = turn_pool.tile([P, PACK, P], F32, name="turned")
+            for t in range(PACK):
+                nc.tensor.transpose(turned[:, t, :], source(t), ident[:])
+            bank[key] = turned
+
+        def turn_scales():
+            turned = turn_pool.tile([P, PACK, P], F32, name="turned")
+            flat = turned[:].rearrange("s t e -> s (t e)")
+            for k in range(B * PACK):
+                b, t = divmod(k, PACK)
+                nc.tensor.transpose(flat[:, 2 * k : 2 * k + P], vs_got[:, b * N + t : (b + 1) * N : PACK], ident[:])
+            bank["vs"] = flat
+
+        def take_scales(engine):
+            source = bank["vs"][:, 0 : 2 * B * PACK : 2]
+            if engine == "S":
+                nc.scalar.activation(vs_cols[:], source, COPY)
+            else:
+                nc.vector.tensor_copy(vs_cols[:], source)
+
+        def load_value_tokens(b, c):
+            a0 = b * SEG + c * (SEG // 2)
+            a1 = a0 + SEG // 2
+            nc.sync.dma_start(v_raw[:, :, a0:a1], vT.rearrange("(h p) n -> p h n", h=2)[:, :, a0:a1])
+
+        def cast_values(b, c):
+            a0 = b * SEG + c * (SEG // 2)
+            a1 = a0 + SEG // 2
+            nc.scalar.activation(v_pairs[:, a0:a1, :], v_raw[:, :, a0:a1].rearrange("p h n -> p n h"), COPY)
+
+        def gather_value_words(b):
+            words = v_pairs[:].rearrange("p n e -> p (n e)").bitcast(U32)
+            window = words[:, 0:SEG] if b == 0 else words
+            nc.vector.tensor_copy(v_words[b][:].rearrange("p t s -> p s t"), window.indirect(listed(b)))
+
+        def turn_value_words(b):
+            turn(("v", b), lambda t: v_words[b][:, t, :].bitcast(F32))
+
+        def settle_value_words(b, h, engine):
+            pairs = bank[("v", b)][:].rearrange("s t p -> s (t p)").bitcast(BF16)
+            pairs = pairs.rearrange("s (t p h) -> s h p t", t=PACK, h=2)
+            if h is None:
+                target, source = v_in[b][:].rearrange("s (h p) t -> s h p t", h=2), pairs
+            else:
+                target, source = v_in[b][:, h * HALF : (h + 1) * HALF, :], pairs[:, h, :, :]
+            if engine == "S":
+                nc.scalar.copy(target, source)
+            else:
+                nc.vector.tensor_copy(target, source)
+
+        def gather_values(b, h):
+            window = v_raw[:, h, 0:SEG] if b == 0 else v_raw[:, h, :]
+            nc.vector.tensor_copy(v_got[b][h][:], window.indirect(listed(b)))
+
+        def turn_values(b, h):
+            turn(("v", b, h), lambda t: v_got[b][h][:, t:N:PACK])
+
+        def settle_values(b, h, e0, e1, engine):
+            target = v_in[b][:, h * HALF + e0 : h * HALF + e1, :]
+            source = bank[("v", b, h)][:, :, e0:e1].rearrange("s t e -> s e t")
+            if engine == "S":
+                nc.scalar.activation(target, source, COPY)
+            else:
+                nc.vector.tensor_copy(target, source)
+
+        def quantize_values(b, e0, e1):
             nc.vector.quantize_mx(
                 out=v_codes[b][:, e0:e1].bitcast(FP8X4),
                 scales=v_scales[b][:, e0:e1],
                 in_=v_in[b][:, e0:e1, :].rearrange("s e t -> s (e t)"),
             )
 
-        k_in = [keep.tile([P, PACK, P, 2], U32, name="k_in%d" % b, align_bytes=64) for b in range(B)]
-        k_codes = [keep.tile([P, N], U32, name="k_codes%d" % b, align_bytes=64) for b in range(B)]
-        k_scales = [keep.tile([P, N], U8, name="k_scales%d" % b, align_bytes=64) for b in range(B)]
-
-        def keys_cast(engine, u, b, a0, a1):
+        def cast_keys(b, u, a0, a1, engine):
             dst = k_pairs[u][:, b * SEG + a0 : b * SEG + a1, :]
-            source = k_raw[u][b][:, :, a0:a1].rearrange("p e n -> p n e")
-            if engine == "scalar":
+            source = k_raw[b][u][:, :, a0:a1].rearrange("p e n -> p n e")
+            if engine == "S":
                 nc.scalar.activation(dst, source, COPY)
             else:
                 nc.vector.tensor_copy(dst, source)
 
-        def keys_got(u, b):
+        def gather_keys(b, u):
             words = k_pairs[u][:].rearrange("p n e -> p (n e)").bitcast(U32)
             window = words[:, 0:SEG] if b == 0 else words
             nc.vector.tensor_copy(k_in[b][:, :, :, u].rearrange("p t s -> p s t"), window.indirect(listed(b)))
 
-        def keys_quantized(b):
+        def quantize_keys(b):
             nc.vector.quantize_mx(
                 out=k_codes[b][:].bitcast(FP8X4),
                 scales=k_scales[b][:],
                 in_=k_in[b][:].rearrange("p t s u -> p (t s u)").bitcast(BF16),
             )
 
-        recip = [keep.tile([P, 1], F32, name="recip%d" % b) for b in range(B)]
-        w_codes = [keep.tile([P, NQ], U32, name="w_codes%d" % b, align_bytes=64) for b in range(B)]
-        w_scales = [keep.tile([P, NQ], U8, name="w_scales%d" % b, align_bytes=64) for b in range(B)]
-
-        def weights(b):
+        def score(b):
             scores = score_pool.tile([P, PACK, NQ], F32, name="scores")
             for t in range(PACK):
                 nc.tensor.matmul_mx(
@@ -150,36 +207,63 @@ def tile_attend_relu2_seg_kernel(tc, qT, kT, vT, vs, offs, out):
                     start=True,
                     stop=True,
                 )
-            scaled = keep.tile([P, PACK, NQ], F32, name="scaled%d" % b)
-            for t in range(PACK):
-                nc.scalar.activation(scaled[:, t, :], scores[:, t, :], COPY, scale=vs_cols[b][:, t : t + 1])
-            w_in = keep.tile([P, NQ, PACK], BF16, name="w_in%d" % b, align_bytes=64)
+            bank[("s", b)] = scores
+
+        def relu(b):
+            nc.scalar.activation(positive[b][:], bank[("s", b)][:], RELU)
+
+        def scale_scores(b, t):
+            nc.scalar.activation(scaled[b][:, t, :], bank[("s", b)][:, t, :], COPY, scale=vs_cols[:, b * PACK + t : b * PACK + t + 1])
+
+        def square(b, engine):
+            if engine == "S":
+                nc.scalar.activation(scaled[b][:], positive[b][:], SQUARE)
+            elif engine == "G":
+                nc.gpsimd.tensor_tensor(scaled[b][:], positive[b][:], positive[b][:], MULT)
+            else:
+                nc.vector.scalar_tensor_tensor(
+                    out=scaled[b][:], in0=bank[("s", b)][:], scalar=0.0, in1=positive[b][:], op0=MAX, op1=MULT
+                )
+
+        def spread(b):
+            return vs_cols[:, b * PACK : (b + 1) * PACK].unsqueeze(1).to_broadcast([P, NQ, PACK])
+
+        def by_query(tile):
+            return tile[:].rearrange("s t q -> s q t")
+
+        def scale_positive(b):
             nc.vector.scalar_tensor_tensor(
-                out=w_in[:],
-                in0=scores[:].rearrange("s t q -> s q t"),
-                scalar=0.0,
-                in1=scaled[:].rearrange("s t q -> s q t"),
-                op0=MAX,
-                op1=MULT,
+                out=by_query(scaled[b]), in0=by_query(bank[("s", b)]), scalar=0.0, in1=spread(b), op0=MAX, op1=MULT
             )
+
+        def weigh(b, form):
+            if form in ("z", "v"):
+                nc.vector.scalar_tensor_tensor(
+                    out=w_in[b][:], in0=by_query(bank[("s", b)]), scalar=0.0, in1=by_query(scaled[b]), op0=MAX, op1=MULT
+                )
+            elif form in ("g", "G"):
+                nc.gpsimd.tensor_tensor(w_in[b][:], by_query(scaled[b]), spread(b), MULT)
+            else:
+                nc.vector.tensor_tensor(w_in[b][:], by_query(scaled[b]), spread(b), MULT)
+
+        def quantize_weights(b):
             nc.vector.quantize_mx(
-                out=w_codes[b][:].bitcast(FP8X4), scales=w_scales[b][:], in_=w_in[:].rearrange("s q t -> s (q t)")
+                out=w_codes[b][:].bitcast(FP8X4), scales=w_scales[b][:], in_=w_in[b][:].rearrange("s q t -> s (q t)")
             )
-            positive = keep.tile([P, PACK, NQ], F32, name="positive%d" % b)
-            nc.scalar.activation(positive[:], scores[:], RELU)
-            turned = turn_pool.tile([P, PACK, P], F32, name="turned")
-            for t in range(PACK):
-                nc.tensor.transpose(turned[:, t, :], positive[:, t, :], ident[:])
-            squares = keep.tile([P, PACK, P], F32, name="squares%d" % b)
-            total = keep.tile([P, 1], F32, name="total%d" % b)
-            nc.scalar.activation(squares[:], turned[:], SQUARE, accum_out=total[:])
-            total1 = keep.tile([P, 1], F32, name="total1%d" % b)
-            nc.vector.tensor_scalar(total1[:], total[:], 1.0, None, op0=ADD)
-            nc.vector.reciprocal(recip[b][:], total1[:])
 
-        y_sb = [keep.tile([P, DV], F32, name="y_sb%d" % b) for b in range(B)]
+        def turn_positive(b):
+            turn(("p", b), lambda t: positive[b][:, t, :])
 
-        def outputs(b, e0, e1):
+        def sum_weights(b):
+            nc.scalar.activation(squares[b][:], bank[("p", b)][:], SQUARE, accum_out=total[b][:])
+
+        def add_one(b):
+            nc.gpsimd.tensor_scalar(total1[b][:], total[b][:], 1.0, None, op0=ADD)
+
+        def invert_total(b):
+            nc.vector.reciprocal(recip[b][:], total1[b][:])
+
+        def multiply_values(b, e0, e1):
             y = y_pool.tile([P, DV], F32, name="y")
             nc.tensor.matmul_mx(
                 out=y[:, 0 : e1 - e0],
@@ -190,37 +274,95 @@ def tile_attend_relu2_seg_kernel(tc, qT, kT, vT, vs, offs, out):
                 start=True,
                 stop=True,
             )
-            nc.scalar.activation(y_sb[b][:, e0:e1], y[:, 0 : e1 - e0], COPY, scale=recip[b][:])
-            nc.sync.dma_start(out[b][:, e0:e1], y_sb[b][:, e0:e1])
+            bank[("y", b, e0)] = y
 
-        H = SEG // 2
-        values_turned(0, 0)
-        scales_of(0)
-        values_turned(0, 1)
-        keys_cast("scalar", 0, 0, 0, H)
-        keys_cast("scalar", 0, 0, H, SEG)
-        keys_got(0, 0)
-        values_quantized(0, 0, DV)
-        keys_cast("scalar", 1, 0, 0, H)
-        keys_cast("scalar", 1, 0, H, H + 192)
-        keys_cast("vector", 1, 0, H + 192, SEG)
-        keys_got(1, 0)
-        keys_quantized(0)
-        scales_of(1)
-        keys_cast("scalar", 0, 1, 0, H)
-        keys_cast("scalar", 0, 1, H, SEG)
-        weights(0)
-        keys_got(0, 1)
-        outputs(0, 0, DV)
-        keys_cast("scalar", 1, 1, 0, H)
-        keys_cast("scalar", 1, 1, H, H + 192)
-        keys_cast("vector", 1, 1, H + 192, SEG)
-        keys_got(1, 1)
-        keys_quantized(1)
-        values_turned(1, 0)
-        weights(1)
-        values_quantized(1, 0, HALF)
-        values_turned(1, 1)
-        values_quantized(1, HALF, DV)
-        outputs(1, 0, HALF)
-        outputs(1, HALF, DV)
+        def settle_output(b, e0, e1):
+            nc.scalar.activation(y_sb[b][:, e0:e1], bank[("y", b, e0)][:, 0 : e1 - e0], COPY, scale=recip[b][:])
+
+        def store_output(b, e0, e1):
+            nc.scalar.dma_start(out[b][:, e0:e1], y_sb[b][:, e0:e1])
+
+        nc.vector.memset(warm[:], 0.0)
+        nc.scalar.activation(warm[:, 4:8], warm[:, 0:4], SQUARE)
+        nc.sync.dma_start(offsets[:], offs)
+        nc.gpsimd.memset(vs_tab[:, 0:1280], 0.0)
+        nc.vector.memset(vs_tab[:, 1280:T], 0.0)
+        load_keys(0, 1, 1)
+        make_identity(nc, ident[:])
+        load_scales()
+        load_keys(0, 1, 0)
+        load_keys(0, 0, 1)
+        cast_keys(0, 1, 512, 1024, "S")
+        gather_scales()
+        load_keys(1, 0, 1)
+        cast_keys(0, 1, 0, 320, "S")
+        load_keys(0, 0, 0)
+        cast_keys(0, 0, 512, 1024, "S")
+        cast_keys(0, 1, 320, 512, "V")
+        load_keys(1, 0, 0)
+        turn_scales()
+        gather_keys(0, 1)
+        load_keys(1, 1, 0)
+        cast_keys(1, 0, 512, 768, "S")
+        cast_keys(1, 0, 768, 1024, "V")
+        cast_keys(0, 0, 0, 320, "S")
+        load_keys(1, 1, 1)
+        cast_keys(0, 0, 320, 512, "V")
+        take_scales("V")
+        cast_keys(1, 0, 0, 384, "S")
+        cast_keys(1, 0, 384, 512, "V")
+        load_queries()
+        gather_keys(0, 0)
+        cast_keys(1, 1, 0, 512, "S")
+        load_value_tokens(0, 0)
+        gather_keys(1, 0)
+        cast_keys(1, 1, 512, 1024, "S")
+        load_value_tokens(0, 1)
+        quantize_keys(0)
+        cast_queries_gpsimd()
+        load_values(1, 0)
+        gather_keys(1, 1)
+        cast_values(0, 0)
+        load_values(1, 1)
+        quantize_queries()
+        cast_values(0, 1)
+        quantize_keys(1)
+        score(0)
+        gather_values(1, 0)
+        score(1)
+        relu(0)
+        relu(1)
+        gather_value_words(0)
+        turn_values(1, 0)
+        square(0, "G")
+        turn_positive(0)
+        settle_values(1, 0, 0, 128, "S")
+        turn_positive(1)
+        gather_values(1, 1)
+        turn_value_words(0)
+        weigh(0, "G")
+        sum_weights(0)
+        settle_value_words(0, None, "S")
+        scale_positive(1)
+        add_one(0)
+        turn_values(1, 1)
+        invert_total(0)
+        weigh(1, "v")
+        sum_weights(1)
+        quantize_values(0, 0, DV)
+        settle_values(1, 1, 0, 128, "S")
+        quantize_weights(0)
+        add_one(1)
+        quantize_weights(1)
+        multiply_values(0, 0, 256)
+        quantize_values(1, 0, 128)
+        settle_output(0, 0, 256)
+        quantize_values(1, 128, 256)
+        multiply_values(1, 0, 128)
+        invert_total(1)
+        multiply_values(1, 128, 256)
+        store_output(0, 0, 256)
+        settle_output(1, 0, 128)
+        settle_output(1, 128, 256)
+        store_output(1, 0, 128)
+        store_output(1, 128, 256)

@@ -54,9 +54,11 @@ def tile_attend_relu2_seg_kernel(tc, qT, kT, vT, vs, offs, out):
         v_scales = [keep.tile([P, DV], U8, name="v_scales%d" % b, align_bytes=64) for b in range(B)]
         v_in = [keep.tile([P, DV, PACK], BF16, name="v_in%d" % b, align_bytes=64) for b in range(B)]
         k_in = [keep.tile([P, PACK, P, 2], U32, name="k_in%d" % b, align_bytes=64) for b in range(B)]
+        k_got = [keep.tile([P, 2, PACK, P], U32, name="k_got%d" % b, align_bytes=64) for b in range(B)]
         k_codes = [keep.tile([P, N], U32, name="k_codes%d" % b, align_bytes=64) for b in range(B)]
         k_scales = [keep.tile([P, N], U8, name="k_scales%d" % b, align_bytes=64) for b in range(B)]
         scaled = [keep.tile([P, PACK, NQ], F32, name="scaled%d" % b) for b in range(B)]
+        shaped = [keep.tile([P, NQ, PACK], F32, name="shaped%d" % b) for b in range(B)]
         positive = [keep.tile([P, PACK, NQ], F32, name="positive%d" % b) for b in range(B)]
         squares = [keep.tile([P, PACK, P], F32, name="squares%d" % b) for b in range(B)]
         w_in = [keep.tile([P, NQ, PACK], BF16, name="w_in%d" % b, align_bytes=64) for b in range(B)]
@@ -81,9 +83,11 @@ def tile_attend_relu2_seg_kernel(tc, qT, kT, vT, vs, offs, out):
         def load_values(b, h):
             nc.sync.dma_start(v_raw[:, h, b * SEG : (b + 1) * SEG], vT[h * P : (h + 1) * P, b * SEG : (b + 1) * SEG])
 
-        def load_keys(b, u, c):
-            a0, a1 = (0, SEG) if c is None else (c * (SEG // 2), (c + 1) * (SEG // 2))
+        def load_keys(b, u, a0, a1):
             nc.sync.dma_start(k_raw[b][u][:, :, a0:a1], kv[:, 2 * u : 2 * u + 2, b * SEG + a0 : b * SEG + a1])
+
+        def load_offsets():
+            nc.sync.dma_start(offsets[:], offs)
 
         def cast_queries(b):
             nc.scalar.activation(q_in[:, b, :, :], q_raw[:, b, :].rearrange("p (j q) -> p q j", j=PACK), COPY)
@@ -123,15 +127,17 @@ def tile_attend_relu2_seg_kernel(tc, qT, kT, vT, vs, offs, out):
             else:
                 nc.vector.tensor_copy(vs_cols[:], source)
 
-        def load_value_tokens(b, c):
-            a0 = b * SEG + c * (SEG // 2)
-            a1 = a0 + SEG // 2
-            nc.sync.dma_start(v_raw[:, :, a0:a1], vT.rearrange("(h p) n -> p h n", h=2)[:, :, a0:a1])
+        def load_value_tokens(b, a0, a1):
+            n0, n1 = b * SEG + a0, b * SEG + a1
+            nc.sync.dma_start(v_raw[:, :, n0:n1], vT.rearrange("(h p) n -> p h n", h=2)[:, :, n0:n1])
 
-        def cast_values(b, c):
-            a0 = b * SEG + c * (SEG // 2)
-            a1 = a0 + SEG // 2
-            nc.scalar.activation(v_pairs[:, a0:a1, :], v_raw[:, :, a0:a1].rearrange("p h n -> p n h"), COPY)
+        def cast_values(b, a0, a1, engine):
+            dst = v_pairs[:, b * SEG + a0 : b * SEG + a1, :]
+            source = v_raw[:, :, b * SEG + a0 : b * SEG + a1].rearrange("p h n -> p n h")
+            if engine == "S":
+                nc.scalar.activation(dst, source, COPY)
+            else:
+                nc.vector.tensor_copy(dst, source)
 
         def gather_value_words(b):
             words = v_pairs[:].rearrange("p n e -> p (n e)").bitcast(U32)
@@ -188,6 +194,19 @@ def tile_attend_relu2_seg_kernel(tc, qT, kT, vT, vs, offs, out):
             window = words[:, 0:SEG] if b == 0 else words
             nc.vector.tensor_copy(k_in[b][:, :, :, u].rearrange("p t s -> p s t"), window.indirect(listed(b)))
 
+        def gather_keys_apart(b, u):
+            words = k_pairs[u][:].rearrange("p n e -> p (n e)").bitcast(U32)
+            window = words[:, 0:SEG] if b == 0 else words
+            nc.vector.tensor_copy(k_got[b][:, u, :, :].rearrange("p t s -> p s t"), window.indirect(listed(b)))
+
+        def lay_keys(b, engine):
+            target = k_in[b][:].rearrange("p t s u -> p (t s) u")
+            source = k_got[b][:].rearrange("p u t s -> p (t s) u")
+            if engine == "V":
+                nc.vector.tensor_copy(target, source)
+            else:
+                nc.gpsimd.tensor_copy(target, source)
+
         def quantize_keys(b):
             nc.vector.quantize_mx(
                 out=k_codes[b][:].bitcast(FP8X4),
@@ -233,11 +252,15 @@ def tile_attend_relu2_seg_kernel(tc, qT, kT, vT, vs, offs, out):
 
         def scale_positive(b):
             nc.vector.scalar_tensor_tensor(
-                out=by_query(scaled[b]), in0=by_query(bank[("s", b)]), scalar=0.0, in1=spread(b), op0=MAX, op1=MULT
+                out=shaped[b][:], in0=by_query(bank[("s", b)]), scalar=0.0, in1=spread(b), op0=MAX, op1=MULT
             )
 
         def weigh(b, form):
-            if form in ("z", "v"):
+            if form == "v":
+                nc.vector.scalar_tensor_tensor(
+                    out=w_in[b][:], in0=by_query(bank[("s", b)]), scalar=0.0, in1=shaped[b][:], op0=MAX, op1=MULT
+                )
+            elif form == "z":
                 nc.vector.scalar_tensor_tensor(
                     out=w_in[b][:], in0=by_query(bank[("s", b)]), scalar=0.0, in1=by_query(scaled[b]), op0=MAX, op1=MULT
                 )
@@ -284,85 +307,87 @@ def tile_attend_relu2_seg_kernel(tc, qT, kT, vT, vs, offs, out):
 
         nc.vector.memset(warm[:], 0.0)
         nc.scalar.activation(warm[:, 4:8], warm[:, 0:4], SQUARE)
-        nc.sync.dma_start(offsets[:], offs)
         nc.gpsimd.memset(vs_tab[:, 0:1280], 0.0)
         nc.vector.memset(vs_tab[:, 1280:T], 0.0)
-        load_keys(0, 1, 1)
+        load_offsets()
+        load_keys(0, 0, 256, 512)
         make_identity(nc, ident[:])
         load_scales()
-        load_keys(0, 1, 0)
-        load_keys(0, 0, 1)
-        cast_keys(0, 1, 512, 1024, "S")
+        load_keys(0, 0, 0, 256)
+        load_keys(0, 0, 512, 1024)
+        load_keys(0, 1, 0, 512)
+        cast_keys(0, 0, 256, 512, "S")
         gather_scales()
-        load_keys(1, 0, 1)
-        cast_keys(0, 1, 0, 320, "S")
-        load_keys(0, 0, 0)
-        cast_keys(0, 0, 512, 1024, "S")
-        cast_keys(0, 1, 320, 512, "V")
-        load_keys(1, 0, 0)
+        cast_keys(0, 0, 0, 256, "S")
+        load_keys(0, 1, 512, 1024)
+        cast_keys(0, 0, 512, 896, "S")
+        load_keys(1, 0, 512, 1024)
+        cast_keys(0, 0, 896, 1024, "V")
         turn_scales()
-        gather_keys(0, 1)
-        load_keys(1, 1, 0)
-        cast_keys(1, 0, 512, 768, "S")
-        cast_keys(1, 0, 768, 1024, "V")
-        cast_keys(0, 0, 0, 320, "S")
-        load_keys(1, 1, 1)
-        cast_keys(0, 0, 320, 512, "V")
+        cast_keys(0, 1, 0, 512, "S")
+        gather_keys_apart(0, 0)
+        load_keys(1, 0, 0, 512)
+        cast_keys(0, 1, 512, 704, "S")
+        load_keys(1, 1, 512, 1024)
+        cast_keys(0, 1, 704, 1024, "V")
+        cast_keys(1, 0, 512, 1024, "S")
         take_scales("V")
+        gather_keys_apart(0, 1)
+        load_keys(1, 1, 0, 512)
         cast_keys(1, 0, 0, 384, "S")
-        cast_keys(1, 0, 384, 512, "V")
         load_queries()
-        gather_keys(0, 0)
-        cast_keys(1, 1, 0, 512, "S")
-        load_value_tokens(0, 0)
-        gather_keys(1, 0)
+        cast_keys(1, 0, 384, 512, "V")
+        lay_keys(0, "V")
         cast_keys(1, 1, 512, 1024, "S")
-        load_value_tokens(0, 1)
-        quantize_keys(0)
+        load_value_tokens(0, 512, 1024)
+        gather_keys_apart(1, 0)
+        load_value_tokens(0, 0, 512)
+        cast_keys(1, 1, 0, 320, "S")
+        cast_keys(1, 1, 320, 512, "V")
         cast_queries_gpsimd()
+        quantize_keys(0)
         load_values(1, 0)
-        gather_keys(1, 1)
-        cast_values(0, 0)
+        gather_keys_apart(1, 1)
+        cast_values(0, 512, 1024, "S")
         load_values(1, 1)
         quantize_queries()
-        cast_values(0, 1)
-        quantize_keys(1)
+        cast_values(0, 0, 320, "S")
+        lay_keys(1, "V")
         score(0)
-        gather_values(1, 0)
-        score(1)
+        cast_values(0, 320, 512, "V")
+        quantize_keys(1)
         relu(0)
-        relu(1)
         gather_value_words(0)
-        turn_values(1, 0)
+        score(1)
         square(0, "G")
         turn_positive(0)
-        settle_values(1, 0, 0, 128, "S")
-        turn_positive(1)
+        relu(1)
         gather_values(1, 1)
         turn_value_words(0)
-        weigh(0, "G")
         sum_weights(0)
-        settle_value_words(0, None, "S")
-        scale_positive(1)
-        add_one(0)
+        turn_positive(1)
+        weigh(0, "G")
+        gather_values(1, 0)
+        square(1, "S")
         turn_values(1, 1)
-        invert_total(0)
-        weigh(1, "v")
-        sum_weights(1)
-        quantize_values(0, 0, DV)
-        settle_values(1, 1, 0, 128, "S")
+        settle_value_words(0, None, "S")
+        settle_values(1, 1, 64, 128, "V")
+        add_one(0)
+        turn_values(1, 0)
         quantize_weights(0)
-        add_one(1)
+        invert_total(0)
+        settle_values(1, 1, 0, 64, "S")
+        weigh(1, "p")
+        settle_values(1, 0, 0, 128, "S")
+        quantize_values(0, 0, DV)
         quantize_weights(1)
+        sum_weights(1)
         multiply_values(0, 0, 256)
-        quantize_values(1, 0, 128)
+        quantize_values(1, 0, 256)
         settle_output(0, 0, 256)
-        quantize_values(1, 128, 256)
-        multiply_values(1, 0, 128)
+        multiply_values(1, 0, 256)
+        add_one(1)
         invert_total(1)
-        multiply_values(1, 128, 256)
+        settle_output(1, 0, 256)
         store_output(0, 0, 256)
-        settle_output(1, 0, 128)
-        settle_output(1, 128, 256)
-        store_output(1, 0, 128)
-        store_output(1, 128, 256)
+        store_output(1, 0, 256)

@@ -310,84 +310,81 @@ def tile_attend_relu2_seg_kernel(tc, qT, kT, vT, vs, offs, out):
         nc.gpsimd.memset(vs_tab[:, 0:1280], 0.0)
         nc.vector.memset(vs_tab[:, 1280:T], 0.0)
         load_offsets()
-        load_keys(0, 0, 256, 512)
+        load_keys(0, 0, 0, 512)
         make_identity(nc, ident[:])
         load_scales()
-        load_keys(0, 0, 0, 256)
         load_keys(0, 0, 512, 1024)
-        load_keys(0, 1, 0, 512)
-        cast_keys(0, 0, 256, 512, "S")
+        load_keys(0, 1, 384, 1024)
+        cast_keys(0, 0, 0, 512, "S")
         gather_scales()
-        cast_keys(0, 0, 0, 256, "S")
-        load_keys(0, 1, 512, 1024)
-        cast_keys(0, 0, 512, 896, "S")
-        load_keys(1, 0, 512, 1024)
-        cast_keys(0, 0, 896, 1024, "V")
+        load_keys(0, 1, 0, 384)
+        load_keys(1, 1, 0, 256)
+        cast_keys(0, 0, 512, 1024, "S")
+        load_keys(1, 0, 384, 1024)
+        cast_keys(0, 1, 384, 784, "S")
+        cast_keys(0, 1, 784, 1024, "V")
         turn_scales()
-        cast_keys(0, 1, 0, 512, "S")
+        load_keys(1, 0, 0, 384)
         gather_keys_apart(0, 0)
-        load_keys(1, 0, 0, 512)
-        cast_keys(0, 1, 512, 704, "S")
-        load_keys(1, 1, 512, 1024)
-        cast_keys(0, 1, 704, 1024, "V")
-        cast_keys(1, 0, 512, 1024, "S")
+        cast_keys(0, 1, 0, 384, "S")
+        load_keys(1, 1, 256, 512)
         take_scales("V")
+        load_keys(1, 1, 512, 1024)
+        cast_keys(1, 1, 0, 256, "S")
         gather_keys_apart(0, 1)
-        load_keys(1, 1, 0, 512)
-        cast_keys(1, 0, 0, 384, "S")
         load_queries()
-        cast_keys(1, 0, 384, 512, "V")
+        cast_keys(1, 0, 384, 1024, "S")
+        cast_keys(1, 0, 144, 384, "V")
         lay_keys(0, "V")
-        cast_keys(1, 1, 512, 1024, "S")
-        load_value_tokens(0, 512, 1024)
-        gather_keys_apart(1, 0)
-        load_value_tokens(0, 0, 512)
-        cast_keys(1, 1, 0, 320, "S")
-        cast_keys(1, 1, 320, 512, "V")
-        cast_queries_gpsimd()
         quantize_keys(0)
-        load_values(1, 0)
-        gather_keys_apart(1, 1)
-        cast_values(0, 512, 1024, "S")
+        load_value_tokens(0, 0, 640)
+        cast_keys(1, 0, 0, 144, "S")
+        load_value_tokens(0, 640, 1024)
+        cast_keys(1, 1, 256, 512, "V")
+        gather_keys_apart(1, 0)
+        cast_queries_gpsimd()
         load_values(1, 1)
+        cast_keys(1, 1, 512, 1024, "S")
+        load_values(1, 0)
+        cast_values(0, 0, 640, "S")
+        gather_keys_apart(1, 1)
         quantize_queries()
-        cast_values(0, 0, 320, "S")
         lay_keys(1, "V")
-        score(0)
-        cast_values(0, 320, 512, "V")
         quantize_keys(1)
+        score(0)
+        cast_values(0, 640, 1024, "S")
+        gather_values(1, 1)
+        score(1)
         relu(0)
         gather_value_words(0)
-        score(1)
+        relu(1)
         square(0, "G")
         turn_positive(0)
-        relu(1)
-        gather_values(1, 1)
-        turn_value_words(0)
+        turn_values(1, 1)
         sum_weights(0)
         turn_positive(1)
-        weigh(0, "G")
         gather_values(1, 0)
+        turn_value_words(0)
         square(1, "S")
-        turn_values(1, 1)
-        settle_value_words(0, None, "S")
-        settle_values(1, 1, 64, 128, "V")
         add_one(0)
-        turn_values(1, 0)
-        quantize_weights(0)
-        invert_total(0)
+        weigh(0, "G")
         settle_values(1, 1, 0, 64, "S")
         weigh(1, "p")
+        turn_values(1, 0)
+        settle_value_words(0, None, "S")
+        invert_total(0)
+        settle_values(1, 1, 64, 128, "V")
+        quantize_weights(1)
+        quantize_weights(0)
         settle_values(1, 0, 0, 128, "S")
         quantize_values(0, 0, DV)
-        quantize_weights(1)
         sum_weights(1)
-        multiply_values(0, 0, 256)
         quantize_values(1, 0, 256)
-        settle_output(0, 0, 256)
+        multiply_values(0, 0, 256)
         multiply_values(1, 0, 256)
+        settle_output(0, 0, 256)
         add_one(1)
         invert_total(1)
-        settle_output(1, 0, 256)
         store_output(0, 0, 256)
+        settle_output(1, 0, 256)
         store_output(1, 0, 256)

from contextlib import ExitStack

import concourse.mybir as mybir
from concourse.masks import make_identity

B, NQ, N, T, D, DV = 2, 128, 512, 2048, 512, 256
P = 128
PACK = 4
SEG = T // B
HALF = DV // 2

F32 = mybir.dt.float32
BF16 = mybir.dt.bfloat16
U32 = mybir.dt.uint32
U16 = mybir.dt.uint16
U8 = mybir.dt.uint8
FP8X4 = mybir.dt.float8_e4m3fn_x4
COPY = mybir.ActivationFunctionType.Copy
RELU = mybir.ActivationFunctionType.Relu
SQUARE = mybir.ActivationFunctionType.Square
ADD = mybir.AluOpType.add
MAX = mybir.AluOpType.max
MULT = mybir.AluOpType.mult

FLOPS = 2 * B * NQ * N * (D + DV)
BYTES = 4 * (B * D * NQ + D * T + DV * T + T + B * NQ * DV) + 2 * P * (B * N // 16)


def tile_attend_relu2_seg_kernel(tc, qT, kT, vT, vs, offs, out):
    nc = tc.nc
    with ExitStack() as ctx:
        keep = ctx.enter_context(tc.tile_pool(name="keep", bufs=1))
        turn_pool = ctx.enter_context(tc.psum_pool(name="turns", bufs=4))
        score_pool = ctx.enter_context(tc.psum_pool(name="scores", bufs=2))
        y_pool = ctx.enter_context(tc.psum_pool(name="ys", bufs=2))

        offsets = keep.tile([P, B * N // 16], U16, name="offsets")
        vs_tab = keep.tile([P, T], F32, name="vs_tab")
        ident = keep.tile([P, P], F32, name="ident")
        warm = keep.tile([P, 8], F32, name="warm")
        q_raw = keep.tile([P, B, PACK * NQ], F32, name="q_raw")
        v_raw = keep.tile([P, 2, T], F32, name="v_raw")
        k_raw = [[keep.tile([P, 2, SEG], F32, name="k_raw%d%d" % (u, b)) for u in range(2)] for b in range(B)]
        k_pairs = [keep.tile([P, T, 2], BF16, name="k_pairs%d" % u, align_bytes=64) for u in range(2)]
        q_in = keep.tile([P, B, NQ, PACK], BF16, name="q_in", align_bytes=64)
        q_codes = keep.tile([P, B * NQ], U32, name="q_codes", align_bytes=64)
        q_scales = keep.tile([P, B * NQ], U8, name="q_scales", align_bytes=64)
        vs_got = keep.tile([P, B * N], F32, name="vs_got")
        vs_cols = keep.tile([P, B * PACK], F32, name="vs_cols")
        v_pairs = keep.tile([P, T, 2], BF16, name="v_pairs", align_bytes=64)
        v_words = [keep.tile([P, PACK, P], U32, name="v_words%d" % b, align_bytes=64) for b in range(B)]
        v_got = [[keep.tile([P, N], F32, name="v_got%d%d" % (b, h)) for h in range(2)] for b in range(B)]
        v_codes = [keep.tile([P, DV], U32, name="v_codes%d" % b, align_bytes=64) for b in range(B)]
        v_scales = [keep.tile([P, DV], U8, name="v_scales%d" % b, align_bytes=64) for b in range(B)]
        v_in = [keep.tile([P, DV, PACK], BF16, name="v_in%d" % b, align_bytes=64) for b in range(B)]
        k_in = [keep.tile([P, PACK, P, 2], U32, name="k_in%d" % b, align_bytes=64) for b in range(B)]
        k_got = [keep.tile([P, 2, PACK, P], U32, name="k_got%d" % b, align_bytes=64) for b in range(B)]
        k_codes = [keep.tile([P, N], U32, name="k_codes%d" % b, align_bytes=64) for b in range(B)]
        k_scales = [keep.tile([P, N], U8, name="k_scales%d" % b, align_bytes=64) for b in range(B)]
        scaled = [keep.tile([P, PACK, NQ], F32, name="scaled%d" % b) for b in range(B)]
        shaped = [keep.tile([P, NQ, PACK], F32, name="shaped%d" % b) for b in range(B)]
        positive = [keep.tile([P, PACK, NQ], F32, name="positive%d" % b) for b in range(B)]
        squares = [keep.tile([P, PACK, P], F32, name="squares%d" % b) for b in range(B)]
        w_in = [keep.tile([P, NQ, PACK], BF16, name="w_in%d" % b, align_bytes=64) for b in range(B)]
        w_codes = [keep.tile([P, NQ], U32, name="w_codes%d" % b, align_bytes=64) for b in range(B)]
        w_scales = [keep.tile([P, NQ], U8, name="w_scales%d" % b, align_bytes=64) for b in range(B)]
        total = [keep.tile([P, 1], F32, name="total%d" % b) for b in range(B)]
        total1 = [keep.tile([P, 1], F32, name="total1%d" % b) for b in range(B)]
        recip = [keep.tile([P, 1], F32, name="recip%d" % b) for b in range(B)]
        y_sb = [keep.tile([P, DV], F32, name="y_sb%d" % b) for b in range(B)]
        bank = {}
        kv = kT.rearrange("(p j) n -> p j n", j=PACK)

        def listed(b):
            return offsets[:, b * (N // 16) : (b + 1) * (N // 16)]

        def load_scales():
            nc.sync.dma_start(vs_tab[0:1, :], vs[0:1, :])

        def load_queries():
            nc.sync.dma_start(q_raw[:], qT.rearrange("b (p j) q -> p b (j q)", j=PACK))

        def load_values(b, h):
            nc.sync.dma_start(v_raw[:, h, b * SEG : (b + 1) * SEG], vT[h * P : (h + 1) * P, b * SEG : (b + 1) * SEG])

        def load_keys(b, u, a0, a1):
            nc.sync.dma_start(k_raw[b][u][:, :, a0:a1], kv[:, 2 * u : 2 * u + 2, b * SEG + a0 : b * SEG + a1])

        def load_offsets():
            nc.sync.dma_start(offsets[:], offs)

        def cast_queries(b):
            nc.scalar.activation(q_in[:, b, :, :], q_raw[:, b, :].rearrange("p (j q) -> p q j", j=PACK), COPY)

        def cast_queries_gpsimd():
            for b in range(B):
                nc.gpsimd.tensor_scalar(
                    q_in[:, b, :, :], q_raw[:, b, :].rearrange("p (j q) -> p q j", j=PACK), 1.0, 0.0, op0=MULT, op1=ADD
                )

        def quantize_queries():
            nc.vector.quantize_mx(
                out=q_codes[:].bitcast(FP8X4), scales=q_scales[:], in_=q_in[:].rearrange("p b q j -> p (b q j)")
            )

        def gather_scales():
            nc.vector.tensor_copy(vs_got[:], vs_tab[:].indirect(offsets[:]))

        def turn(key, source):
            turned = turn_pool.tile([P, PACK, P], F32, name="turned")
            for t in range(PACK):
                nc.tensor.transpose(turned[:, t, :], source(t), ident[:])
            bank[key] = turned

        def turn_scales():
            turned = turn_pool.tile([P, PACK, P], F32, name="turned")
            flat = turned[:].rearrange("s t e -> s (t e)")
            for k in range(B * PACK):
                b, t = divmod(k, PACK)
                nc.tensor.transpose(flat[:, 2 * k : 2 * k + P], vs_got[:, b * N + t : (b + 1) * N : PACK], ident[:])
            bank["vs"] = flat

        def take_scales(engine):
            source = bank["vs"][:, 0 : 2 * B * PACK : 2]
            if engine == "S":
                nc.scalar.activation(vs_cols[:], source, COPY)
            else:
                nc.vector.tensor_copy(vs_cols[:], source)

        def load_value_tokens(b, a0, a1):
            n0, n1 = b * SEG + a0, b * SEG + a1
            nc.sync.dma_start(v_raw[:, :, n0:n1], vT.rearrange("(h p) n -> p h n", h=2)[:, :, n0:n1])

        def cast_values(b, a0, a1, engine):
            dst = v_pairs[:, b * SEG + a0 : b * SEG + a1, :]
            source = v_raw[:, :, b * SEG + a0 : b * SEG + a1].rearrange("p h n -> p n h")
            if engine == "S":
                nc.scalar.activation(dst, source, COPY)
            else:
                nc.vector.tensor_copy(dst, source)

        def gather_value_words(b):
            words = v_pairs[:].rearrange("p n e -> p (n e)").bitcast(U32)
            window = words[:, 0:SEG] if b == 0 else words
            nc.vector.tensor_copy(v_words[b][:].rearrange("p t s -> p s t"), window.indirect(listed(b)))

        def turn_value_words(b):
            turn(("v", b), lambda t: v_words[b][:, t, :].bitcast(F32))

        def settle_value_words(b, h, engine):
            pairs = bank[("v", b)][:].rearrange("s t p -> s (t p)").bitcast(BF16)
            pairs = pairs.rearrange("s (t p h) -> s h p t", t=PACK, h=2)
            if h is None:
                target, source = v_in[b][:].rearrange("s (h p) t -> s h p t", h=2), pairs
            else:
                target, source = v_in[b][:, h * HALF : (h + 1) * HALF, :], pairs[:, h, :, :]
            if engine == "S":
                nc.scalar.copy(target, source)
            else:
                nc.vector.tensor_copy(target, source)

        def gather_values(b, h):
            window = v_raw[:, h, 0:SEG] if b == 0 else v_raw[:, h, :]
            nc.vector.tensor_copy(v_got[b][h][:], window.indirect(listed(b)))

        def turn_values(b, h):
            turn(("v", b, h), lambda t: v_got[b][h][:, t:N:PACK])

        def settle_values(b, h, e0, e1, engine):
            target = v_in[b][:, h * HALF + e0 : h * HALF + e1, :]
            source = bank[("v", b, h)][:, :, e0:e1].rearrange("s t e -> s e t")
            if engine == "S":
                nc.scalar.activation(target, source, COPY)
            else:
                nc.vector.tensor_copy(target, source)

        def quantize_values(b, e0, e1):
            nc.vector.quantize_mx(
                out=v_codes[b][:, e0:e1].bitcast(FP8X4),
                scales=v_scales[b][:, e0:e1],
                in_=v_in[b][:, e0:e1, :].rearrange("s e t -> s (e t)"),
            )

        def cast_keys(b, u, a0, a1, engine):
            dst = k_pairs[u][:, b * SEG + a0 : b * SEG + a1, :]
            source = k_raw[b][u][:, :, a0:a1].rearrange("p e n -> p n e")
            if engine == "S":
                nc.scalar.activation(dst, source, COPY)
            else:
                nc.vector.tensor_copy(dst, source)

        def gather_keys(b, u):
            words = k_pairs[u][:].rearrange("p n e -> p (n e)").bitcast(U32)
            window = words[:, 0:SEG] if b == 0 else words
            nc.vector.tensor_copy(k_in[b][:, :, :, u].rearrange("p t s -> p s t"), window.indirect(listed(b)))

        def gather_keys_apart(b, u):
            words = k_pairs[u][:].rearrange("p n e -> p (n e)").bitcast(U32)
            window = words[:, 0:SEG] if b == 0 else words
            nc.vector.tensor_copy(k_got[b][:, u, :, :].rearrange("p t s -> p s t"), window.indirect(listed(b)))

        def lay_keys(b, engine):
            target = k_in[b][:].rearrange("p t s u -> p (t s) u")
            source = k_got[b][:].rearrange("p u t s -> p (t s) u")
            if engine == "V":
                nc.vector.tensor_copy(target, source)
            else:
                nc.gpsimd.tensor_copy(target, source)

        def quantize_keys(b):
            nc.vector.quantize_mx(
                out=k_codes[b][:].bitcast(FP8X4),
                scales=k_scales[b][:],
                in_=k_in[b][:].rearrange("p t s u -> p (t s u)").bitcast(BF16),
            )

        def score(b):
            scores = score_pool.tile([P, PACK, NQ], F32, name="scores")
            for t in range(PACK):
                nc.tensor.matmul_mx(
                    out=scores[:, t, :],
                    lhsT=k_codes[b][:, t * P : (t + 1) * P].bitcast(FP8X4),
                    lhsT_scale=k_scales[b][:, t * P : (t + 1) * P],
                    rhs=q_codes[:, b * NQ : (b + 1) * NQ].bitcast(FP8X4),
                    rhs_scale=q_scales[:, b * NQ : (b + 1) * NQ],
                    start=True,
                    stop=True,
                )
            bank[("s", b)] = scores

        def relu(b):
            nc.scalar.activation(positive[b][:], bank[("s", b)][:], RELU)

        def scale_scores(b, t):
            nc.scalar.activation(scaled[b][:, t, :], bank[("s", b)][:, t, :], COPY, scale=vs_cols[:, b * PACK + t : b * PACK + t + 1])

        def square(b, engine):
            if engine == "S":
                nc.scalar.activation(scaled[b][:], positive[b][:], SQUARE)
            elif engine == "G":
                nc.gpsimd.tensor_tensor(scaled[b][:], positive[b][:], positive[b][:], MULT)
            else:
                nc.vector.scalar_tensor_tensor(
                    out=scaled[b][:], in0=bank[("s", b)][:], scalar=0.0, in1=positive[b][:], op0=MAX, op1=MULT
                )

        def spread(b):
            return vs_cols[:, b * PACK : (b + 1) * PACK].unsqueeze(1).to_broadcast([P, NQ, PACK])

        def by_query(tile):
            return tile[:].rearrange("s t q -> s q t")

        def scale_positive(b):
            nc.vector.scalar_tensor_tensor(
                out=shaped[b][:], in0=by_query(bank[("s", b)]), scalar=0.0, in1=spread(b), op0=MAX, op1=MULT
            )

        def weigh(b, form):
            if form == "v":
                nc.vector.scalar_tensor_tensor(
                    out=w_in[b][:], in0=by_query(bank[("s", b)]), scalar=0.0, in1=shaped[b][:], op0=MAX, op1=MULT
                )
            elif form == "z":
                nc.vector.scalar_tensor_tensor(
                    out=w_in[b][:], in0=by_query(bank[("s", b)]), scalar=0.0, in1=by_query(scaled[b]), op0=MAX, op1=MULT
                )
            elif form in ("g", "G"):
                nc.gpsimd.tensor_tensor(w_in[b][:], by_query(scaled[b]), spread(b), MULT)
            else:
                nc.vector.tensor_tensor(w_in[b][:], by_query(scaled[b]), spread(b), MULT)

        def quantize_weights(b):
            nc.vector.quantize_mx(
                out=w_codes[b][:].bitcast(FP8X4), scales=w_scales[b][:], in_=w_in[b][:].rearrange("s q t -> s (q t)")
            )

        def turn_positive(b):
            turn(("p", b), lambda t: positive[b][:, t, :])

        def sum_weights(b):
            nc.scalar.activation(squares[b][:], bank[("p", b)][:], SQUARE, accum_out=total[b][:])

        def add_one(b):
            nc.gpsimd.tensor_scalar(total1[b][:], total[b][:], 1.0, None, op0=ADD)

        def invert_total(b):
            nc.vector.reciprocal(recip[b][:], total1[b][:])

        def multiply_values(b, e0, e1):
            y = y_pool.tile([P, DV], F32, name="y")
            nc.tensor.matmul_mx(
                out=y[:, 0 : e1 - e0],
                lhsT=w_codes[b][:].bitcast(FP8X4),
                lhsT_scale=w_scales[b][:],
                rhs=v_codes[b][:, e0:e1].bitcast(FP8X4),
                rhs_scale=v_scales[b][:, e0:e1],
                start=True,
                stop=True,
            )
            bank[("y", b, e0)] = y

        def settle_output(b, e0, e1):
            nc.scalar.activation(y_sb[b][:, e0:e1], bank[("y", b, e0)][:, 0 : e1 - e0], COPY, scale=recip[b][:])

        def store_output(b, e0, e1):
            nc.scalar.dma_start(out[b][:, e0:e1], y_sb[b][:, e0:e1])

        nc.vector.memset(warm[:], 0.0)
        nc.scalar.activation(warm[:, 4:8], warm[:, 0:4], SQUARE)
        nc.gpsimd.memset(vs_tab[:, 0:1280], 0.0)
        nc.vector.memset(vs_tab[:, 1280:T], 0.0)
        load_offsets()
        load_keys(0, 0, 0, 512)
        make_identity(nc, ident[:])
        load_scales()
        load_keys(0, 0, 512, 1024)
        load_keys(0, 1, 384, 1024)
        cast_keys(0, 0, 0, 512, "S")
        gather_scales()
        load_keys(0, 1, 0, 384)
        load_keys(1, 1, 0, 256)
        cast_keys(0, 0, 512, 1024, "S")
        load_keys(1, 0, 384, 1024)
        cast_keys(0, 1, 384, 784, "S")
        cast_keys(0, 1, 784, 1024, "V")
        turn_scales()
        load_keys(1, 0, 0, 384)
        gather_keys_apart(0, 0)
        cast_keys(0, 1, 0, 384, "S")
        load_keys(1, 1, 256, 512)
        take_scales("V")
        load_keys(1, 1, 512, 1024)
        cast_keys(1, 1, 0, 256, "S")
        gather_keys_apart(0, 1)
        load_queries()
        cast_keys(1, 0, 384, 1024, "S")
        cast_keys(1, 0, 144, 384, "V")
        lay_keys(0, "V")
        quantize_keys(0)
        load_value_tokens(0, 0, 640)
        cast_keys(1, 0, 0, 144, "S")
        load_value_tokens(0, 640, 1024)
        cast_keys(1, 1, 256, 512, "V")
        gather_keys_apart(1, 0)
        cast_queries_gpsimd()
        load_values(1, 1)
        cast_keys(1, 1, 512, 1024, "S")
        load_values(1, 0)
        cast_values(0, 0, 640, "S")
        gather_keys_apart(1, 1)
        quantize_queries()
        lay_keys(1, "V")
        quantize_keys(1)
        score(0)
        cast_values(0, 640, 1024, "S")
        gather_values(1, 1)
        score(1)
        relu(0)
        gather_value_words(0)
        relu(1)
        square(0, "G")
        turn_positive(0)
        turn_values(1, 1)
        sum_weights(0)
        turn_positive(1)
        gather_values(1, 0)
        turn_value_words(0)
        square(1, "S")
        add_one(0)
        weigh(0, "G")
        settle_values(1, 1, 0, 64, "S")
        weigh(1, "p")
        turn_values(1, 0)
        settle_value_words(0, None, "S")
        invert_total(0)
        settle_values(1, 1, 64, 128, "V")
        quantize_weights(1)
        quantize_weights(0)
        settle_values(1, 0, 0, 128, "S")
        quantize_values(0, 0, DV)
        sum_weights(1)
        quantize_values(1, 0, 256)
        multiply_values(0, 0, 256)
        multiply_values(1, 0, 256)
        settle_output(0, 0, 256)
        add_one(1)
        invert_total(1)
        store_output(0, 0, 256)
        settle_output(1, 0, 256)
        store_output(1, 0, 256)
